import numpy as np, ml_dtypes
CORES = [24,40,56,80,88,96]
N = 6
import mx_ref
NC, KT, WT = 512, 4, 1
BF = ml_dtypes.bfloat16
def cut(t, i, w=512):
    return t[:, w * i:w * i + w]
def pk(c, s, i=0):
    return (np.ascontiguousarray(c[:, 512 * i:512 * i + 512]), mx_ref.live(s[:, 128 * i:128 * i + 128]))
def inputs(rng, e, E):
    def f(*shape):
        v = (rng.standard_normal(shape, dtype=np.float32) * np.exp2(rng.integers(-2, 3, shape[:-1] + (1,)))).astype(BF)
        return mx_ref.spread((v.astype(np.float32) * np.exp2(rng.integers(-E, E + 1, shape[:-2] + (1, 1))).astype(np.float32)).astype(BF), rng, e)
    def packed(k):
        c = np.zeros((N, 128, k * 512), np.uint8); s = np.zeros((N, 128, k * 128), np.uint8)
        for r in range(N):
            for i in range(k):
                a, b = mx_ref.quantize(f(128, 512)); c[r][:, 512 * i:512 * i + 512] = a; s[r][:, 128 * i:128 * i + 128] = mx_ref.plane(b, rng)
        return c, s
    d = {}
    d["wc"], d["ws"] = packed(KT * WT)
    d["x"] = f(N, 128, KT * 4 * NC)
    return d
def setup_inputs(rng):
    return inputs(rng, 0, 0)
def setup_inputs_blocks(rng):
    return inputs(rng, 2, 0)
def setup_inputs_wide(rng):
    d = inputs(rng, 0, 1); d["x"] = inputs(rng, 0, 0)["x"]
    return d
def reference(wc, ws, x):
    X = [[mx_ref.quantize(cut(x[j], t, 4 * NC)) for t in range(KT)] for j in range(N)]
    y = np.zeros((N, 128, N * WT * NC), np.float32)
    for r in range(N):
        for b in range(N * WT):
            j, i = divmod(b, WT)
            for t in range(KT):
                p = mx_ref.matmul(pk(wc[r], ws[r], KT * i + t), X[j][t])
                z = p if t == 0 else z + p
            y[r][:, NC * b:NC * b + NC] = z
    return {"y": y}

@@ -1,0 +1,321 @@
+from concourse.bass import DstId, RemoteDMATransfer
+from concourse.mybir import dt
+
+N, NT, NC = 6, 4, 512
+SIM = 112
+HALF = NC // 2
+SLOTS = 7
+XS, YS = 4, 5
+OPT = dict(quota=8,
+           two=(1, 3),
+           step=3.0, lag=3.0, hop=6.0, relay=2.0,
+           seeds=100, order=None, fm=None)
+
+SCRATCH = {
+    "wq": ("sbuf", [128, NT * 128], "float8_e4m3fn_x4"),
+    "wp": ("sbuf", [128, NT * 128], "uint8"),
+    "xs": ("sbuf", [128, XS * 4 * HALF], "bfloat16"),
+    "qc": ("sbuf", [128, SLOTS * NC], "float8_e4m3fn_x4"),
+    "qp": ("sbuf", [128, SLOTS * NC], "uint8"),
+    "ys": ("sbuf", [128, YS * HALF], "float32"),
+    "ps": ("psum", [128, NC * N], "float32"),
+}
+for _s in range(N):
+    for _t in range(NT):
+        SCRATCH["c%d_%d" % (_s, _t)] = ("dram", [128, NC], "float8_e4m3fn_x4")
+        SCRATCH["p%d_%d" % (_s, _t)] = ("dram", [128, NC], "uint8")
+
+SEMAPHORES = (["a%d_%d" % (s, t) for s in range(N) for t in range(NT)]
+              + ["u%d" % p for p in range(2 * NT)] + ["x%d" % p for p in range(XS)] + ["w", "out", "csent"]
+              + ["f%d" % k for k in range(SLOTS)] + ["m%d" % k for k in range(SLOTS)] + ["cr%d" % k for k in range(SLOTS)]
+              + ["v%d" % k for k in range(YS)] + ["st%d" % k for k in range(YS)]
+              + ["sent%d" % t for t in range(NT)])
+
+_PLAN = {}
+
+
+def bits(m):
+    return bin(m).count("1")
+
+
+def make_plan(T, topo):
+    if _PLAN:
+        return _PLAN
+    cores = list(T.cores)
+    on_chip = {}
+    for c in range(SIM):
+        on_chip.setdefault(topo.chip(c), []).append(c)
+    mate = {a: b for a in on_chip for b in on_chip if topo.mates(a, b)}
+    rank_on = {topo.chip(c): r for r, c in enumerate(cores)}
+    chips = [topo.chip(c) for c in cores]
+
+    def lane(s, t):
+        home = topo.die(cores[s])
+        return home if t % 2 == 0 else [topo.die(c) for c in on_chip[chips[s]] if topo.die(c) != home][0]
+
+    def owns_port(c):
+        return topo.may_write(c, on_chip[mate[topo.chip(c)]][0])
+
+    def port(ch, s, t):
+        return [c for c in on_chip[ch] if topo.die(c) == lane(s, t) and owns_port(c)][t // 2]
+
+    def receiver(r, s, t):
+        q = [c for c in on_chip[chips[r]] if topo.die(c) == lane(s, t) and not owns_port(c) and c != cores[r]]
+        return q[(t // 2) % len(q)]
+
+    def links(a, b):
+        at, to, d = topo.chip(a), topo.chip(b), topo.die(a)
+        way = []
+        if at != to and not topo.same_plane(at, to):
+            way.append(("mate", at, d))
+            at = mate[at]
+        if at != to:
+            way += [("out", at, d), ("in", to, d)]
+        return way
+
+    relayed = set()
+    for r in range(N):
+        peer = rank_on.get(mate[chips[r]])
+        left = OPT["quota"] - (NT if peer is not None else 0)
+        cross = [s for s in range(N) if s != r and s != peer and not topo.same_plane(chips[s], chips[r])]
+        busy = [s for s in cross if mate[chips[s]] in rank_on]
+        free = [s for s in cross if s not in busy]
+        order = [(s, t) for s in busy for t in range(NT)]
+        order += [(free[(t + r + k) % len(free)], t) for k in range(len(free)) for t in range(NT)]
+        for s, t in order[:left]:
+            relayed.add((s, t, r))
+
+    flows, served, first = [], {}, {}
+    for s in range(N):
+        for t in range(NT):
+            p = port(chips[s], s, t)
+            for r in range(N):
+                if (s, t, r) in relayed:
+                    peer = rank_on.get(mate[chips[r]])
+                    served[(s, t, port(mate[chips[r]], s, t))] = [r] + ([peer] if peer is not None and peer != s else [])
+            via = [v for (a, b, v) in served if (a, b) == (s, t)]
+            hit = [r for v in via for r in served[(s, t, v)]]
+            for d in via + [cores[r] for r in range(N) if r != s and r not in hit]:
+                q = receiver(s, s, t) if t in OPT["two"] and topo.same_plane(topo.chip(d), chips[s]) else p
+                flows.append((s, t, q, d, links(q, d)))
+                if q not in first.setdefault((s, t), []):
+                    first[(s, t)].append(q)
+
+    def schedule(seed):
+        todo, z, got = list(flows), 0, []
+        while todo:
+            load, left = {}, {}
+            for s, t, p, d, way in todo:
+                left[p] = left.get(p, 0) + 1
+                for l in way:
+                    load[l] = load.get(l, 0) + 1
+
+            def rate(f):
+                s, t, p, d, way = f
+                h = (seed * 7919 + s * 31 + t * 17 + d * 13 + z * 101) * 2654435761 % 4294967296 / 4294967296.0
+                return -(max(load[l] for l in way) + left[p] + (1.5 if (s, t, d) in served else 0) + 1.5 * h)
+            todo.sort(key=rate)
+            used = set()
+            for shared in range(2):
+                rest = []
+                for f in todo:
+                    s, t, p, d, way = f
+                    if z < t // 2 or p in used or any(l in used for l in way if not (shared and l[0] == "out")):
+                        rest.append(f)
+                        continue
+                    used.add(p)
+                    used.update(way)
+                    got.append((z, s, t, p, d))
+                todo = rest
+            z += 1
+        return (z, sum(x[0] * (2 if (x[1], x[2], x[4]) in served else 1) for x in got), seed), got
+
+    best = min((schedule(seed) for seed in range(OPT["seeds"])), key=lambda v: v[0])
+    sends = []
+    last = {}
+    for z, s, t, p, d in best[1]:
+        key = OPT["step"] * (z + 1) + OPT["lag"] * t
+        via = served.get((s, t, d))
+        sends.append((key - 100, p, s, t, d, None if via else T.rank_of(d)))
+        if via:
+            for j, q in enumerate(via):
+                last[(s, t, q)] = (d, key + OPT["hop"] + OPT["relay"] * j)
+                sends.append((key + OPT["relay"] * j, d, s, t, cores[q], q))
+        else:
+            last[(s, t, T.rank_of(d))] = (p, key)
+    order = OPT["order"] or {r: [(s, t) for key, s, t in sorted((last[(s, t, r)][1], s, t) for s in range(N)
+                                                                 for t in range(NT) if s != r)] for r in range(N)}
+    land = {}
+    for r in range(N):
+        user = [("own", t) for t in range(NT)] + [None] * (SLOTS - NT)
+        rot = list(range(NT, SLOTS)) + list(range(NT))
+        for i, (s, t) in enumerate(order[r]):
+            f, k = last[(s, t, r)][0], rot[i % SLOTS]
+            fetch = topo.chip(f) == chips[r] or (OPT["fm"] and OPT["fm"](i, s, t))
+            land[(s, t, r)] = dict(mode="fetch" if fetch else "push", slot=k, before=user[k], via=f if fetch else receiver(r, s, t))
+            user[k] = (s, t)
+    jobs = {}
+    size = {}
+    for key, p, s, t, d, r in sends:
+        if r is not None and land[(s, t, r)]["mode"] == "push":
+            q = land[(s, t, r)]["via"]
+            jobs.setdefault(q, []).append((order[r].index((s, t)), s, t, d, land[(s, t, r)]["slot"], r))
+            size[(s, t, d)] = 2 * bits(topo.mask(q, d))
+            d = q
+        jobs.setdefault(p, []).append((key, s, t, d, None, None))
+        size[(s, t, d)] = 2 * bits(topo.mask(p, d))
+    for s, t in first:
+        for p in first[(s, t)]:
+            size[(s, t, p)] = 2 * bits(topo.mask(cores[s], p))
+    for c in jobs:
+        jobs[c].sort(key=lambda j: j[0])
+    _PLAN.update(dict(jobs=jobs, size=size, order=order, land=land, last=last, first=first, span=best[0]))
+    return _PLAN
+
+
+def rank_program(g, core, T, topo):
+    plan = make_plan(T, topo)
+    rank = T.rank_of(core)
+    if rank is not None:
+        member(g, core, rank, T, topo, plan)
+    elif core in plan["jobs"]:
+        helper(g, core, T, topo, plan)
+
+
+def codes_of(T, s, t):
+    return T["c%d_%d" % (s, t)][:].bitcast(dt.uint8)
+
+
+def plane_of(T, s, t):
+    return T["p%d_%d" % (s, t)][:]
+
+
+def slot_codes(T, k):
+    return T.qc[:, k * NC:(k + 1) * NC].bitcast(dt.uint8)
+
+
+def slot_plane(T, k):
+    return T.qp[:, k * NC:(k + 1) * NC]
+
+
+def send(g, core, T, topo, s, t, d, src, dst, local):
+    arr = T.sem["a%d_%d" % (s, t)]
+    rid, pid, _e = topo.addr(d)
+    m = topo.mask(core, d)
+    for whole, part in ((plane_of(T, s, t), slot_plane), (codes_of(T, s, t), slot_codes)):
+        g.remote_dma(whole if dst is None else part(T, dst), whole if src is None else part(T, src), arr, local, pid, rid, m)
+    return 2 * bits(m)
+
+
+def helper(g, core, T, topo, plan):
+    total, have, credit = 0, set(), {}
+    for key, s, t, d, k, r in plan["jobs"][core]:
+        if (s, t) not in have:
+            have.add((s, t))
+            g.wait_ge(T.sem["a%d_%d" % (s, t)], plan["size"][(s, t, core)])
+        if r is not None and plan["land"][(s, t, r)]["before"] is not None:
+            credit[k] = credit.get(k, 0) + 1
+            g.wait_ge(T.sem["cr%d" % k], credit[k])
+        total += send(g, core, T, topo, s, t, d, None, k, T.sem.out)
+    g.wait_ge(T.sem.out, total)
+
+
+def member(g, core, rank, T, topo, plan):
+    load = [g.sync, g.scalar]
+    w = 4 * HALF
+    for p in range(2 * NT):
+        q, k = load[p % 2], p % XS
+        if p >= XS:
+            q.wait_ge(T.sem["u%d" % (p - XS)], 1)
+        q.dma_start(T.xs[:, k * w:(k + 1) * w], T.x[:, p * w:(p + 1) * w]).then_inc(T.sem["x%d" % k], 16)
+    g.scalar.dma_start(T.wq[:].bitcast(dt.uint8), T.wc[:]).then_inc(T.sem.w, 16)
+    g.scalar.dma_start(T.wp[:], T.ws[:]).then_inc(T.sem.w, 16)
+    for p in range(2 * NT):
+        k = p % XS
+        g.vector.wait_ge(T.sem["x%d" % k], 16 * (p // XS + 1))
+        a = p * HALF
+        g.vector.quantize_mx(T.qc[:, a:a + HALF], T.qp[:, a:a + HALF], T.xs[:, k * w:(k + 1) * w]).then_inc(T.sem["u%d" % p], 1)
+    sent = [0] * NT
+    for t in range(NT):
+        g.wait_ge(T.sem["u%d" % (2 * t)], 1)
+        g.wait_ge(T.sem["u%d" % (2 * t + 1)], 1)
+        for p in plan["first"][(rank, t)]:
+            sent[t] += send(g, core, T, topo, rank, t, p, t, None, T.sem["sent%d" % t])
+
+    uses = [0] * SLOTS
+    fetches = [0] * SLOTS
+    ny = [0]
+    csent = [0]
+
+    def multiply(k, j, t, first, last):
+        g.tensor.matmul_mx(T.ps[:, j * NC:(j + 1) * NC], T.wq[:, t * 128:(t + 1) * 128], T.wp[:, t * 128:(t + 1) * 128],
+                           T.qc[:, k * NC:(k + 1) * NC], T.qp[:, k * NC:(k + 1) * NC], first, last).then_inc(T.sem["m%d" % k], 1)
+        uses[k] += 1
+
+    def drain(j, k):
+        g.vector.wait_ge(T.sem["m%d" % k], uses[k])
+        for h in range(2):
+            i, e = ny[0] % YS, ny[0] // YS
+            if e:
+                g.vector.wait_ge(T.sem["st%d" % i], 16 * e)
+            c = j * NC + h * HALF
+            g.vector.tensor_copy(T.ys[:, i * HALF:(i + 1) * HALF], T.ps[:, c:c + HALF]).then_inc(T.sem["v%d" % i], 1)
+            g.scalar.wait_ge(T.sem["v%d" % i], e + 1)
+            g.scalar.dma_start(T.y[:, c:c + HALF], T.ys[:, i * HALF:(i + 1) * HALF]).then_inc(T.sem["st%d" % i], 16)
+            ny[0] += 1
+
+    nexts = {}
+    for s, t in plan["order"][rank]:
+        how = plan["land"][(s, t, rank)]
+        if how["before"] is not None:
+            nexts[how["before"]] = how
+
+    def release(tag, k):
+        how = nexts.get(tag)
+        if how is not None and how["mode"] == "push":
+            if tag[0] == "own":
+                g.wait_ge(T.sem["sent%d" % tag[1]], sent[tag[1]])
+            g.wait_ge(T.sem["m%d" % k], uses[k])
+            rid, pid, _e = topo.addr(how["via"])
+            one = topo.mask(core, how["via"])
+            one &= -one
+            g.remote_sem_update(T.sem["cr%d" % k], T.sem.csent, pid, rid, one)
+            csent[0] += 1
+
+    g.tensor.wait_ge(T.sem.w, 32)
+    for t in range(NT):
+        g.tensor.wait_ge(T.sem["u%d" % (2 * t)], 1)
+        g.tensor.wait_ge(T.sem["u%d" % (2 * t + 1)], 1)
+        multiply(t, rank, t, t == 0, t == NT - 1)
+        release(("own", t), t)
+    drain(rank, NT - 1)
+    got = [0] * N
+    for s, t in plan["order"][rank]:
+        how = plan["land"][(s, t, rank)]
+        k, arr, need = how["slot"], T.sem["a%d_%d" % (s, t)], plan["size"][(s, t, core)]
+        if how["mode"] == "fetch":
+            if how["before"] is not None:
+                if how["before"][0] == "own":
+                    g.sync.wait_ge(T.sem["sent%d" % k], sent[k])
+                g.sync.wait_ge(T.sem["m%d" % k], uses[k])
+            g.sync.wait_ge(arr, need)
+            g.sync.dma_start(slot_codes(T, k), codes_of(T, s, t)).then_inc(T.sem["f%d" % k], 16)
+            g.sync.dma_start(slot_plane(T, k), plane_of(T, s, t)).then_inc(T.sem["f%d" % k], 16)
+            fetches[k] += 32
+            g.tensor.wait_ge(T.sem["f%d" % k], fetches[k])
+        else:
+            g.tensor.wait_ge(arr, need)
+        got[s] += 1
+        multiply(k, s, t, got[s] == 1, got[s] == NT)
+        if got[s] == NT:
+            drain(s, k)
+        release((s, t), k)
+    if csent[0]:
+        g.wait_ge(T.sem.csent, csent[0])
+    for t in range(NT):
+        g.wait_ge(T.sem["sent%d" % t], sent[t])
+    for k in range(SLOTS):
+        g.sync.wait_ge(T.sem["m%d" % k], uses[k])
+    for i in range(YS):
+        n = len([q for q in range(ny[0]) if q % YS == i])
+        g.scalar.wait_ge(T.sem["st%d" % i], 16 * n)

@@ -1,15 +1,15 @@
-from concourse.bass import DstId, RemoteDMATransfer
 from concourse.mybir import dt
 
 N, NT, NC = 6, 4, 512
 SIM = 112
 HALF = NC // 2
-SLOTS = 7
-XS, YS = 4, 5
+SLOTS = 8
+XS, YS = 3, 4
+NB = 28
 OPT = dict(quota=8,
-           two=(1, 3),
-           step=3.0, lag=3.0, hop=6.0, relay=2.0,
-           seeds=100, order=None, fm=None)
+           lag=2,
+           bonus=1.0,
+           seed=73971)
 
 SCRATCH = {
     "wq": ("sbuf", [128, NT * 128], "float8_e4m3fn_x4"),
@@ -20,12 +20,11 @@ SCRATCH = {
     "ys": ("sbuf", [128, YS * HALF], "float32"),
     "ps": ("psum", [128, NC * N], "float32"),
 }
-for _s in range(N):
-    for _t in range(NT):
-        SCRATCH["c%d_%d" % (_s, _t)] = ("dram", [128, NC], "float8_e4m3fn_x4")
-        SCRATCH["p%d_%d" % (_s, _t)] = ("dram", [128, NC], "uint8")
+for _i in range(NB):
+    SCRATCH["hc%d" % _i] = ("dram", [128, HALF], "float8_e4m3fn_x4")
+    SCRATCH["hp%d" % _i] = ("dram", [128, HALF], "uint8")
 
-SEMAPHORES = (["a%d_%d" % (s, t) for s in range(N) for t in range(NT)]
+SEMAPHORES = (["a%d_%d" % (s, t) for s in range(N) for t in range(NT)] + ["b%d" % i for i in range(NB)]
               + ["u%d" % p for p in range(2 * NT)] + ["x%d" % p for p in range(XS)] + ["w", "out", "csent"]
               + ["f%d" % k for k in range(SLOTS)] + ["m%d" % k for k in range(SLOTS)] + ["cr%d" % k for k in range(SLOTS)]
               + ["v%d" % k for k in range(YS)] + ["st%d" % k for k in range(YS)]
@@ -49,28 +48,28 @@ def make_plan(T, topo):
     rank_on = {topo.chip(c): r for r, c in enumerate(cores)}
     chips = [topo.chip(c) for c in cores]
 
-    def lane(s, t):
-        home = topo.die(cores[s])
-        return home if t % 2 == 0 else [topo.die(c) for c in on_chip[chips[s]] if topo.die(c) != home][0]
-
     def owns_port(c):
         return topo.may_write(c, on_chip[mate[topo.chip(c)]][0])
 
-    def port(ch, s, t):
-        return [c for c in on_chip[ch] if topo.die(c) == lane(s, t) and owns_port(c)][t // 2]
+    def lane(s, t, h):
+        home = topo.die(cores[s])
+        return home if (h + t // 2) % 2 == 0 else [topo.die(c) for c in on_chip[chips[s]] if topo.die(c) != home][0]
 
-    def receiver(r, s, t):
-        q = [c for c in on_chip[chips[r]] if topo.die(c) == lane(s, t) and not owns_port(c) and c != cores[r]]
-        return q[(t // 2) % len(q)]
+    def port(ch, die, i):
+        q = [c for c in on_chip[ch] if topo.die(c) == die and owns_port(c)]
+        return q[i % len(q)]
 
-    def links(a, b):
-        at, to, d = topo.chip(a), topo.chip(b), topo.die(a)
+    receivers = [sorted((c for c in on_chip[chips[r]] if not owns_port(c) and c != cores[r]),
+                        key=lambda c: topo.die(c) != topo.die(cores[r])) for r in range(N)]
+
+    def links(a, ch):
+        at, d = topo.chip(a), topo.die(a)
         way = []
-        if at != to and not topo.same_plane(at, to):
+        if at != ch and not topo.same_plane(at, ch):
             way.append(("mate", at, d))
             at = mate[at]
-        if at != to:
-            way += [("out", at, d), ("in", to, d)]
+        if at != ch:
+            way += [("out", at, d), ("in", ch, d)]
         return way
 
     relayed = set()
@@ -80,96 +79,118 @@ def make_plan(T, topo):
         cross = [s for s in range(N) if s != r and s != peer and not topo.same_plane(chips[s], chips[r])]
         busy = [s for s in cross if mate[chips[s]] in rank_on]
         free = [s for s in cross if s not in busy]
-        order = [(s, t) for s in busy for t in range(NT)]
+        order = [(s, t) for t in range(NT) for s in busy]
         order += [(free[(t + r + k) % len(free)], t) for k in range(len(free)) for t in range(NT)]
         for s, t in order[:left]:
             relayed.add((s, t, r))
 
-    flows, served, first = [], {}, {}
+    def flow(s, t, qs, ch, relays, serves, at):
+        return dict(s=s, t=t, qs=qs, ch=ch, relays=relays, serves=serves, way=[l for q in qs for l in links(q, ch)], at=at)
+
+    flows, hand = [], {}
     for s in range(N):
         for t in range(NT):
-            p = port(chips[s], s, t)
+            qs = [port(chips[s], lane(s, t, h), t % 2) for h in range(2)]
+            for h in range(2):
+                hand[(s, t, h)] = qs[h]
+            via, hit = {}, set()
             for r in range(N):
                 if (s, t, r) in relayed:
                     peer = rank_on.get(mate[chips[r]])
-                    served[(s, t, port(mate[chips[r]], s, t))] = [r] + ([peer] if peer is not None and peer != s else [])
-            via = [v for (a, b, v) in served if (a, b) == (s, t)]
-            hit = [r for v in via for r in served[(s, t, v)]]
-            for d in via + [cores[r] for r in range(N) if r != s and r not in hit]:
-                q = receiver(s, s, t) if t in OPT["two"] and topo.same_plane(topo.chip(d), chips[s]) else p
-                flows.append((s, t, q, d, links(q, d)))
-                if q not in first.setdefault((s, t), []):
-                    first[(s, t)].append(q)
+                    via[mate[chips[r]]] = [r] + ([peer] if peer is not None and peer != s else [])
+            for v in via:
+                hit.update(via[v])
+            for ch in via:
+                flows.append(flow(s, t, qs, ch, [port(ch, lane(s, t, h), t + s) for h in range(2)], via[ch], t))
+            for r in range(N):
+                if r != s and r not in hit:
+                    flows.append(flow(s, t, qs, chips[r], None, [], t))
 
     def schedule(seed):
         todo, z, got = list(flows), 0, []
         while todo:
-            load, left = {}, {}
-            for s, t, p, d, way in todo:
-                left[p] = left.get(p, 0) + 1
-                for l in way:
+            load = {}
+            for f in todo:
+                for l in f["qs"] + f["way"]:
                     load[l] = load.get(l, 0) + 1
 
             def rate(f):
-                s, t, p, d, way = f
-                h = (seed * 7919 + s * 31 + t * 17 + d * 13 + z * 101) * 2654435761 % 4294967296 / 4294967296.0
-                return -(max(load[l] for l in way) + left[p] + (1.5 if (s, t, d) in served else 0) + 1.5 * h)
+                h = (seed * 7919 + f["s"] * 31 + f["t"] * 17 + f["ch"] * 13 + z * 101) * 2654435761 % 4294967296 / 4294967296.0
+                return -(max([load[l] for l in f["way"]] + [0]) + load[f["qs"][0]] + (OPT["bonus"] if f["serves"] else 0) + 1.5 * h)
             todo.sort(key=rate)
-            used = set()
+            new, used = [], set()
             for shared in range(2):
                 rest = []
                 for f in todo:
-                    s, t, p, d, way = f
-                    if z < t // 2 or p in used or any(l in used for l in way if not (shared and l[0] == "out")):
+                    if z < f["at"] or any(l in used for l in f["qs"] + [l for l in f["way"] if not (shared and l[0] == "out")]):
                         rest.append(f)
                         continue
-                    used.add(p)
-                    used.update(way)
-                    got.append((z, s, t, p, d))
+                    used.update(f["qs"] + f["way"])
+                    got.append((z, f))
+                    for r in f["serves"]:
+                        new.append(flow(f["s"], f["t"], f["relays"], chips[r], None, [], z + OPT["lag"]))
                 todo = rest
+            todo += new
             z += 1
-        return (z, sum(x[0] * (2 if (x[1], x[2], x[4]) in served else 1) for x in got), seed), got
+        return got
 
-    best = min((schedule(seed) for seed in range(OPT["seeds"])), key=lambda v: v[0])
-    sends = []
-    last = {}
-    for z, s, t, p, d in best[1]:
-        key = OPT["step"] * (z + 1) + OPT["lag"] * t
-        via = served.get((s, t, d))
-        sends.append((key - 100, p, s, t, d, None if via else T.rank_of(d)))
-        if via:
-            for j, q in enumerate(via):
-                last[(s, t, q)] = (d, key + OPT["hop"] + OPT["relay"] * j)
-                sends.append((key + OPT["relay"] * j, d, s, t, cores[q], q))
-        else:
-            last[(s, t, T.rank_of(d))] = (p, key)
-    order = OPT["order"] or {r: [(s, t) for key, s, t in sorted((last[(s, t, r)][1], s, t) for s in range(N)
-                                                                 for t in range(NT) if s != r)] for r in range(N)}
-    land = {}
+    steps = schedule(OPT["seed"])
+    come, source = {r: {} for r in range(N)}, {}
+    for z, f in steps:
+        if not f["serves"]:
+            r = rank_on[f["ch"]]
+            source[(f["s"], f["t"], r)] = f["qs"][0]
+            come[r][(f["s"], f["t"])] = z + (1 if topo.chip(f["qs"][0]) == f["ch"] else 0)
+    land, order = {}, {}
     for r in range(N):
+        order[r] = sorted(come[r], key=lambda v: (come[r][v], v))
         user = [("own", t) for t in range(NT)] + [None] * (SLOTS - NT)
         rot = list(range(NT, SLOTS)) + list(range(NT))
+        n = 0
         for i, (s, t) in enumerate(order[r]):
-            f, k = last[(s, t, r)][0], rot[i % SLOTS]
-            fetch = topo.chip(f) == chips[r] or (OPT["fm"] and OPT["fm"](i, s, t))
-            land[(s, t, r)] = dict(mode="fetch" if fetch else "push", slot=k, before=user[k], via=f if fetch else receiver(r, s, t))
+            k = rot[i % SLOTS]
+            how = dict(mode="fetch", slot=k, before=user[k])
+            if topo.chip(source[(s, t, r)]) != chips[r]:
+                how["mode"] = "push"
+                how["via"] = receivers[r][n % len(receivers[r])]
+                n += 1
+            land[(s, t, r)] = how
             user[k] = (s, t)
+    place, used = {}, {}
     jobs = {}
     size = {}
-    for key, p, s, t, d, r in sends:
-        if r is not None and land[(s, t, r)]["mode"] == "push":
-            q = land[(s, t, r)]["via"]
-            jobs.setdefault(q, []).append((order[r].index((s, t)), s, t, d, land[(s, t, r)]["slot"], r))
-            size[(s, t, d)] = 2 * bits(topo.mask(q, d))
-            d = q
-        jobs.setdefault(p, []).append((key, s, t, d, None, None))
-        size[(s, t, d)] = 2 * bits(topo.mask(p, d))
-    for s, t in first:
-        for p in first[(s, t)]:
-            size[(s, t, p)] = 2 * bits(topo.mask(cores[s], p))
+
+    def buf(p, c):
+        if (p, c) not in place:
+            place[(p, c)] = used.get(c, 0)
+            used[c] = used.get(c, 0) + 1
+        return place[(p, c)]
+
+    def job(q, key, p, d, b, k, sem, credit):
+        jobs.setdefault(q, []).append((key, p, d, b, k, sem, credit))
+        size[(d, sem)] = size.get((d, sem), 0) + 2 * bits(topo.mask(q, d))
+    for p in hand:
+        b = buf(p, hand[p])
+        size[(hand[p], "b%d" % b)] = 2 * bits(topo.mask(cores[p[0]], hand[p]))
+    for z, f in steps:
+        s, t = f["s"], f["t"]
+        for h in range(2):
+            p, q = (s, t, h), f["qs"][h]
+            if f["serves"]:
+                d = f["relays"][h]
+                b = buf(p, d)
+                job(q, z, p, d, b, None, "b%d" % b, False)
+                continue
+            r = rank_on[f["ch"]]
+            how = land[(s, t, r)]
+            d = cores[r] if how["mode"] == "fetch" else how["via"]
+            b = buf(p, d)
+            job(q, z, p, d, b, None, "b%d" % b, False)
+            if how["mode"] == "push":
+                job(d, order[r].index((s, t)), p, cores[r], None, how["slot"], "a%d_%d" % (s, t), how["before"] is not None)
     for c in jobs:
         jobs[c].sort(key=lambda j: j[0])
-    _PLAN.update(dict(jobs=jobs, size=size, order=order, land=land, last=last, first=first, span=best[0]))
+    _PLAN.update(dict(jobs=jobs, size=size, order=order, land=land, hand=hand, place=place))
     return _PLAN
 
 
@@ -182,41 +203,36 @@ def rank_program(g, core, T, topo):
         helper(g, core, T, topo, plan)
 
 
-def codes_of(T, s, t):
-    return T["c%d_%d" % (s, t)][:].bitcast(dt.uint8)
+def park(T, b):
+    return T["hp%d" % b][:], T["hc%d" % b][:].bitcast(dt.uint8)
 
 
-def plane_of(T, s, t):
-    return T["p%d_%d" % (s, t)][:]
+def slot(T, k, h):
+    a = k * NC + h * HALF
+    return T.qp[:, a:a + HALF], T.qc[:, a:a + HALF].bitcast(dt.uint8)
 
 
-def slot_codes(T, k):
-    return T.qc[:, k * NC:(k + 1) * NC].bitcast(dt.uint8)
-
-
-def slot_plane(T, k):
-    return T.qp[:, k * NC:(k + 1) * NC]
-
-
-def send(g, core, T, topo, s, t, d, src, dst, local):
-    arr = T.sem["a%d_%d" % (s, t)]
+def send(g, core, topo, d, src, dst, arr, local):
     rid, pid, _e = topo.addr(d)
     m = topo.mask(core, d)
-    for whole, part in ((plane_of(T, s, t), slot_plane), (codes_of(T, s, t), slot_codes)):
-        g.remote_dma(whole if dst is None else part(T, dst), whole if src is None else part(T, src), arr, local, pid, rid, m)
+    for i, o in zip(src, dst):
+        g.remote_dma(o, i, arr, local, pid, rid, m)
     return 2 * bits(m)
 
 
 def helper(g, core, T, topo, plan):
-    total, have, credit = 0, set(), {}
-    for key, s, t, d, k, r in plan["jobs"][core]:
-        if (s, t) not in have:
-            have.add((s, t))
-            g.wait_ge(T.sem["a%d_%d" % (s, t)], plan["size"][(s, t, core)])
-        if r is not None and plan["land"][(s, t, r)]["before"] is not None:
+    total, have, credit, given = 0, set(), {}, set()
+    for key, p, d, b, k, sem, wants in plan["jobs"][core]:
+        mine = plan["place"][(p, core)]
+        if p not in have:
+            have.add(p)
+            g.wait_ge(T.sem["b%d" % mine], plan["size"][(core, "b%d" % mine)])
+        if wants and p[:2] not in given:
+            given.add(p[:2])
             credit[k] = credit.get(k, 0) + 1
             g.wait_ge(T.sem["cr%d" % k], credit[k])
-        total += send(g, core, T, topo, s, t, d, None, k, T.sem.out)
+        dst = park(T, b) if k is None else slot(T, k, p[2])
+        total += send(g, core, topo, d, park(T, mine), dst, T.sem[sem], T.sem.out)
     g.wait_ge(T.sem.out, total)
 
 
@@ -237,10 +253,11 @@ def member(g, core, rank, T, topo, plan):
         g.vector.quantize_mx(T.qc[:, a:a + HALF], T.qp[:, a:a + HALF], T.xs[:, k * w:(k + 1) * w]).then_inc(T.sem["u%d" % p], 1)
     sent = [0] * NT
     for t in range(NT):
-        g.wait_ge(T.sem["u%d" % (2 * t)], 1)
-        g.wait_ge(T.sem["u%d" % (2 * t + 1)], 1)
-        for p in plan["first"][(rank, t)]:
-            sent[t] += send(g, core, T, topo, rank, t, p, t, None, T.sem["sent%d" % t])
+        for h in range(2):
+            g.wait_ge(T.sem["u%d" % (2 * t + h)], 1)
+            d = plan["hand"][(rank, t, h)]
+            b = plan["place"][((rank, t, h), d)]
+            sent[t] += send(g, core, topo, d, slot(T, t, h), park(T, b), T.sem["b%d" % b], T.sem["sent%d" % t])
 
     uses = [0] * SLOTS
     fetches = [0] * SLOTS
@@ -292,19 +309,22 @@ def member(g, core, rank, T, topo, plan):
     got = [0] * N
     for s, t in plan["order"][rank]:
         how = plan["land"][(s, t, rank)]
-        k, arr, need = how["slot"], T.sem["a%d_%d" % (s, t)], plan["size"][(s, t, core)]
+        k = how["slot"]
         if how["mode"] == "fetch":
             if how["before"] is not None:
                 if how["before"][0] == "own":
                     g.sync.wait_ge(T.sem["sent%d" % k], sent[k])
                 g.sync.wait_ge(T.sem["m%d" % k], uses[k])
-            g.sync.wait_ge(arr, need)
-            g.sync.dma_start(slot_codes(T, k), codes_of(T, s, t)).then_inc(T.sem["f%d" % k], 16)
-            g.sync.dma_start(slot_plane(T, k), plane_of(T, s, t)).then_inc(T.sem["f%d" % k], 16)
-            fetches[k] += 32
+            for h in range(2):
+                b = plan["place"][((s, t, h), core)]
+                g.sync.wait_ge(T.sem["b%d" % b], plan["size"][(core, "b%d" % b)])
+                for o, i in zip(slot(T, k, h), park(T, b)):
+                    g.sync.dma_start(o, i).then_inc(T.sem["f%d" % k], 16)
+                    fetches[k] += 16
             g.tensor.wait_ge(T.sem["f%d" % k], fetches[k])
         else:
-            g.tensor.wait_ge(arr, need)
+            arr = "a%d_%d" % (s, t)
+            g.tensor.wait_ge(T.sem[arr], plan["size"][(core, arr)])
         got[s] += 1
         multiply(k, s, t, got[s] == 1, got[s] == NT)
         if got[s] == NT:

from concourse.mybir import dt

N, NT, NC = 6, 4, 512
SIM = 112
HALF = NC // 2
SLOTS = 8
XS, YS = 3, 4
NB = 28
OPT = dict(quota=8,
           lag=2,
           bonus=1.0,
           seed=73971)

SCRATCH = {
    "wq": ("sbuf", [128, NT * 128], "float8_e4m3fn_x4"),
    "wp": ("sbuf", [128, NT * 128], "uint8"),
    "xs": ("sbuf", [128, XS * 4 * HALF], "bfloat16"),
    "qc": ("sbuf", [128, SLOTS * NC], "float8_e4m3fn_x4"),
    "qp": ("sbuf", [128, SLOTS * NC], "uint8"),
    "ys": ("sbuf", [128, YS * HALF], "float32"),
    "ps": ("psum", [128, NC * N], "float32"),
}
for _i in range(NB):
    SCRATCH["hc%d" % _i] = ("dram", [128, HALF], "float8_e4m3fn_x4")
    SCRATCH["hp%d" % _i] = ("dram", [128, HALF], "uint8")

SEMAPHORES = (["a%d_%d" % (s, t) for s in range(N) for t in range(NT)] + ["b%d" % i for i in range(NB)]
              + ["u%d" % p for p in range(2 * NT)] + ["x%d" % p for p in range(XS)] + ["w", "out", "csent"]
              + ["f%d" % k for k in range(SLOTS)] + ["m%d" % k for k in range(SLOTS)] + ["cr%d" % k for k in range(SLOTS)]
              + ["v%d" % k for k in range(YS)] + ["st%d" % k for k in range(YS)]
              + ["sent%d" % t for t in range(NT)])

_PLAN = {}


def bits(m):
    return bin(m).count("1")


def make_plan(T, topo):
    if _PLAN:
        return _PLAN
    cores = list(T.cores)
    on_chip = {}
    for c in range(SIM):
        on_chip.setdefault(topo.chip(c), []).append(c)
    mate = {a: b for a in on_chip for b in on_chip if topo.mates(a, b)}
    rank_on = {topo.chip(c): r for r, c in enumerate(cores)}
    chips = [topo.chip(c) for c in cores]

    def owns_port(c):
        return topo.may_write(c, on_chip[mate[topo.chip(c)]][0])

    def lane(s, t, h):
        home = topo.die(cores[s])
        return home if (h + t // 2) % 2 == 0 else [topo.die(c) for c in on_chip[chips[s]] if topo.die(c) != home][0]

    def port(ch, die, i):
        q = [c for c in on_chip[ch] if topo.die(c) == die and owns_port(c)]
        return q[i % len(q)]

    receivers = [sorted((c for c in on_chip[chips[r]] if not owns_port(c) and c != cores[r]),
                        key=lambda c: topo.die(c) != topo.die(cores[r])) for r in range(N)]

    def links(a, ch):
        at, d = topo.chip(a), topo.die(a)
        way = []
        if at != ch and not topo.same_plane(at, ch):
            way.append(("mate", at, d))
            at = mate[at]
        if at != ch:
            way += [("out", at, d), ("in", ch, d)]
        return way

    relayed = set()
    for r in range(N):
        peer = rank_on.get(mate[chips[r]])
        left = OPT["quota"] - (NT if peer is not None else 0)
        cross = [s for s in range(N) if s != r and s != peer and not topo.same_plane(chips[s], chips[r])]
        busy = [s for s in cross if mate[chips[s]] in rank_on]
        free = [s for s in cross if s not in busy]
        order = [(s, t) for t in range(NT) for s in busy]
        order += [(free[(t + r + k) % len(free)], t) for k in range(len(free)) for t in range(NT)]
        for s, t in order[:left]:
            relayed.add((s, t, r))

    def flow(s, t, qs, ch, relays, serves, at):
        return dict(s=s, t=t, qs=qs, ch=ch, relays=relays, serves=serves, way=[l for q in qs for l in links(q, ch)], at=at)

    flows, hand = [], {}
    for s in range(N):
        for t in range(NT):
            qs = [port(chips[s], lane(s, t, h), t % 2) for h in range(2)]
            for h in range(2):
                hand[(s, t, h)] = qs[h]
            via, hit = {}, set()
            for r in range(N):
                if (s, t, r) in relayed:
                    peer = rank_on.get(mate[chips[r]])
                    via[mate[chips[r]]] = [r] + ([peer] if peer is not None and peer != s else [])
            for v in via:
                hit.update(via[v])
            for ch in via:
                flows.append(flow(s, t, qs, ch, [port(ch, lane(s, t, h), t + s) for h in range(2)], via[ch], t))
            for r in range(N):
                if r != s and r not in hit:
                    flows.append(flow(s, t, qs, chips[r], None, [], t))

    def schedule(seed):
        todo, z, got = list(flows), 0, []
        while todo:
            load = {}
            for f in todo:
                for l in f["qs"] + f["way"]:
                    load[l] = load.get(l, 0) + 1

            def rate(f):
                h = (seed * 7919 + f["s"] * 31 + f["t"] * 17 + f["ch"] * 13 + z * 101) * 2654435761 % 4294967296 / 4294967296.0
                return -(max([load[l] for l in f["way"]] + [0]) + load[f["qs"][0]] + (OPT["bonus"] if f["serves"] else 0) + 1.5 * h)
            todo.sort(key=rate)
            new, used = [], set()
            for shared in range(2):
                rest = []
                for f in todo:
                    if z < f["at"] or any(l in used for l in f["qs"] + [l for l in f["way"] if not (shared and l[0] == "out")]):
                        rest.append(f)
                        continue
                    used.update(f["qs"] + f["way"])
                    got.append((z, f))
                    for r in f["serves"]:
                        new.append(flow(f["s"], f["t"], f["relays"], chips[r], None, [], z + OPT["lag"]))
                todo = rest
            todo += new
            z += 1
        return got

    steps = schedule(OPT["seed"])
    come, source = {r: {} for r in range(N)}, {}
    for z, f in steps:
        if not f["serves"]:
            r = rank_on[f["ch"]]
            source[(f["s"], f["t"], r)] = f["qs"][0]
            come[r][(f["s"], f["t"])] = z + (1 if topo.chip(f["qs"][0]) == f["ch"] else 0)
    land, order = {}, {}
    for r in range(N):
        order[r] = sorted(come[r], key=lambda v: (come[r][v], v))
        user = [("own", t) for t in range(NT)] + [None] * (SLOTS - NT)
        rot = list(range(NT, SLOTS)) + list(range(NT))
        n = 0
        for i, (s, t) in enumerate(order[r]):
            k = rot[i % SLOTS]
            how = dict(mode="fetch", slot=k, before=user[k])
            if topo.chip(source[(s, t, r)]) != chips[r]:
                how["mode"] = "push"
                how["via"] = receivers[r][n % len(receivers[r])]
                n += 1
            land[(s, t, r)] = how
            user[k] = (s, t)
    place, used = {}, {}
    jobs = {}
    size = {}

    def buf(p, c):
        if (p, c) not in place:
            place[(p, c)] = used.get(c, 0)
            used[c] = used.get(c, 0) + 1
        return place[(p, c)]

    def job(q, key, p, d, b, k, sem, credit):
        jobs.setdefault(q, []).append((key, p, d, b, k, sem, credit))
        size[(d, sem)] = size.get((d, sem), 0) + 2 * bits(topo.mask(q, d))
    for p in hand:
        b = buf(p, hand[p])
        size[(hand[p], "b%d" % b)] = 2 * bits(topo.mask(cores[p[0]], hand[p]))
    for z, f in steps:
        s, t = f["s"], f["t"]
        for h in range(2):
            p, q = (s, t, h), f["qs"][h]
            if f["serves"]:
                d = f["relays"][h]
                b = buf(p, d)
                job(q, z, p, d, b, None, "b%d" % b, False)
                continue
            r = rank_on[f["ch"]]
            how = land[(s, t, r)]
            d = cores[r] if how["mode"] == "fetch" else how["via"]
            b = buf(p, d)
            job(q, z, p, d, b, None, "b%d" % b, False)
            if how["mode"] == "push":
                job(d, order[r].index((s, t)), p, cores[r], None, how["slot"], "a%d_%d" % (s, t), how["before"] is not None)
    for c in jobs:
        jobs[c].sort(key=lambda j: j[0])
    _PLAN.update(dict(jobs=jobs, size=size, order=order, land=land, hand=hand, place=place))
    return _PLAN


def rank_program(g, core, T, topo):
    plan = make_plan(T, topo)
    rank = T.rank_of(core)
    if rank is not None:
        member(g, core, rank, T, topo, plan)
    elif core in plan["jobs"]:
        helper(g, core, T, topo, plan)


def park(T, b):
    return T["hp%d" % b][:], T["hc%d" % b][:].bitcast(dt.uint8)


def slot(T, k, h):
    a = k * NC + h * HALF
    return T.qp[:, a:a + HALF], T.qc[:, a:a + HALF].bitcast(dt.uint8)


def send(g, core, topo, d, src, dst, arr, local):
    rid, pid, _e = topo.addr(d)
    m = topo.mask(core, d)
    for i, o in zip(src, dst):
        g.remote_dma(o, i, arr, local, pid, rid, m)
    return 2 * bits(m)


def helper(g, core, T, topo, plan):
    total, have, credit, given = 0, set(), {}, set()
    for key, p, d, b, k, sem, wants in plan["jobs"][core]:
        mine = plan["place"][(p, core)]
        if p not in have:
            have.add(p)
            g.wait_ge(T.sem["b%d" % mine], plan["size"][(core, "b%d" % mine)])
        if wants and p[:2] not in given:
            given.add(p[:2])
            credit[k] = credit.get(k, 0) + 1
            g.wait_ge(T.sem["cr%d" % k], credit[k])
        dst = park(T, b) if k is None else slot(T, k, p[2])
        total += send(g, core, topo, d, park(T, mine), dst, T.sem[sem], T.sem.out)
    g.wait_ge(T.sem.out, total)


def member(g, core, rank, T, topo, plan):
    load = [g.sync, g.scalar]
    w = 4 * HALF
    for p in range(2 * NT):
        q, k = load[p % 2], p % XS
        if p >= XS:
            q.wait_ge(T.sem["u%d" % (p - XS)], 1)
        q.dma_start(T.xs[:, k * w:(k + 1) * w], T.x[:, p * w:(p + 1) * w]).then_inc(T.sem["x%d" % k], 16)
    g.scalar.dma_start(T.wq[:].bitcast(dt.uint8), T.wc[:]).then_inc(T.sem.w, 16)
    g.scalar.dma_start(T.wp[:], T.ws[:]).then_inc(T.sem.w, 16)
    for p in range(2 * NT):
        k = p % XS
        g.vector.wait_ge(T.sem["x%d" % k], 16 * (p // XS + 1))
        a = p * HALF
        g.vector.quantize_mx(T.qc[:, a:a + HALF], T.qp[:, a:a + HALF], T.xs[:, k * w:(k + 1) * w]).then_inc(T.sem["u%d" % p], 1)
    sent = [0] * NT
    for t in range(NT):
        for h in range(2):
            g.wait_ge(T.sem["u%d" % (2 * t + h)], 1)
            d = plan["hand"][(rank, t, h)]
            b = plan["place"][((rank, t, h), d)]
            sent[t] += send(g, core, topo, d, slot(T, t, h), park(T, b), T.sem["b%d" % b], T.sem["sent%d" % t])

    uses = [0] * SLOTS
    fetches = [0] * SLOTS
    ny = [0]
    csent = [0]

    def multiply(k, j, t, first, last):
        g.tensor.matmul_mx(T.ps[:, j * NC:(j + 1) * NC], T.wq[:, t * 128:(t + 1) * 128], T.wp[:, t * 128:(t + 1) * 128],
                           T.qc[:, k * NC:(k + 1) * NC], T.qp[:, k * NC:(k + 1) * NC], first, last).then_inc(T.sem["m%d" % k], 1)
        uses[k] += 1

    def drain(j, k):
        g.vector.wait_ge(T.sem["m%d" % k], uses[k])
        for h in range(2):
            i, e = ny[0] % YS, ny[0] // YS
            if e:
                g.vector.wait_ge(T.sem["st%d" % i], 16 * e)
            c = j * NC + h * HALF
            g.vector.tensor_copy(T.ys[:, i * HALF:(i + 1) * HALF], T.ps[:, c:c + HALF]).then_inc(T.sem["v%d" % i], 1)
            g.scalar.wait_ge(T.sem["v%d" % i], e + 1)
            g.scalar.dma_start(T.y[:, c:c + HALF], T.ys[:, i * HALF:(i + 1) * HALF]).then_inc(T.sem["st%d" % i], 16)
            ny[0] += 1

    nexts = {}
    for s, t in plan["order"][rank]:
        how = plan["land"][(s, t, rank)]
        if how["before"] is not None:
            nexts[how["before"]] = how

    def release(tag, k):
        how = nexts.get(tag)
        if how is not None and how["mode"] == "push":
            if tag[0] == "own":
                g.wait_ge(T.sem["sent%d" % tag[1]], sent[tag[1]])
            g.wait_ge(T.sem["m%d" % k], uses[k])
            rid, pid, _e = topo.addr(how["via"])
            one = topo.mask(core, how["via"])
            one &= -one
            g.remote_sem_update(T.sem["cr%d" % k], T.sem.csent, pid, rid, one)
            csent[0] += 1

    g.tensor.wait_ge(T.sem.w, 32)
    for t in range(NT):
        g.tensor.wait_ge(T.sem["u%d" % (2 * t)], 1)
        g.tensor.wait_ge(T.sem["u%d" % (2 * t + 1)], 1)
        multiply(t, rank, t, t == 0, t == NT - 1)
        release(("own", t), t)
    drain(rank, NT - 1)
    got = [0] * N
    for s, t in plan["order"][rank]:
        how = plan["land"][(s, t, rank)]
        k = how["slot"]
        if how["mode"] == "fetch":
            if how["before"] is not None:
                if how["before"][0] == "own":
                    g.sync.wait_ge(T.sem["sent%d" % k], sent[k])
                g.sync.wait_ge(T.sem["m%d" % k], uses[k])
            for h in range(2):
                b = plan["place"][((s, t, h), core)]
                g.sync.wait_ge(T.sem["b%d" % b], plan["size"][(core, "b%d" % b)])
                for o, i in zip(slot(T, k, h), park(T, b)):
                    g.sync.dma_start(o, i).then_inc(T.sem["f%d" % k], 16)
                    fetches[k] += 16
            g.tensor.wait_ge(T.sem["f%d" % k], fetches[k])
        else:
            arr = "a%d_%d" % (s, t)
            g.tensor.wait_ge(T.sem[arr], plan["size"][(core, arr)])
        got[s] += 1
        multiply(k, s, t, got[s] == 1, got[s] == NT)
        if got[s] == NT:
            drain(s, k)
        release((s, t), k)
    if csent[0]:
        g.wait_ge(T.sem.csent, csent[0])
    for t in range(NT):
        g.wait_ge(T.sem["sent%d" % t], sent[t])
    for k in range(SLOTS):
        g.sync.wait_ge(T.sem["m%d" % k], uses[k])
    for i in range(YS):
        n = len([q for q in range(ny[0]) if q % YS == i])
        g.scalar.wait_ge(T.sem["st%d" % i], 16 * n)
